import numpy as np
import ml_dtypes


def mxq(x, axis, fmt="e4m3"):
    dtype, down = {"e4m3": (ml_dtypes.float8_e4m3fn, 7), "e5m2": (ml_dtypes.float8_e5m2, 14)}[fmt]
    v = np.moveaxis(np.asarray(x, np.float32).astype(ml_dtypes.bfloat16).astype(np.float64), axis, -1)
    blocks = v.reshape(v.shape[:-1] + (-1, 32))
    amax = np.abs(blocks).max(-1, keepdims=True)
    byte = np.maximum(np.where(amax > 0, np.frexp(amax)[1] - 1 + 127, 0) - down, 1)
    scale = np.exp2(byte - 127.0)
    codes = (blocks / scale).astype(np.float32).astype(dtype).astype(np.float64)
    return np.moveaxis((codes * scale).reshape(v.shape), -1, axis)


WIDE = False


def mx_kscale(k):
    if not WIDE:
        return np.ones(k)
    levels = np.array([10, -10, 5, -5, 0])
    if k % 512:
        return np.exp2(np.random.permutation(np.resize(levels, k // 32))).repeat(32)
    a = np.empty((k // 512, 16))
    for p in range(k // 512):
        a[p, :8] = np.random.permutation(np.resize(levels, 8))
        for g in range(8):
            far = levels[np.abs(levels - a[p, g]) >= 10]
            a[p, g + 8] = far[np.random.randint(len(far))]
    return np.exp2(a.ravel()).repeat(32)


def f64(x):
    return np.asarray(x).astype(np.float64)


def striped(idx):
    return np.tile(idx.reshape(-1, 16).T, (8, 1)).astype(np.uint16)


def unstriped(offs):
    return offs[:16].T.reshape(-1).astype(np.int64)


E2M1 = np.array([0.0, 0.5, 1.0, 1.5, 2.0, 3.0, 4.0, 6.0, -0.0, -0.5, -1.0, -1.5, -2.0, -3.0, -4.0, -6.0])


def pack_weight(w, fmt):
    k, n = w.shape
    w = f64(np.asarray(w, np.float32).astype(ml_dtypes.bfloat16)).reshape(k // 32, 32, n)
    amax = np.abs(w).max(1)
    if fmt == "e4m3":
        byte = np.frexp(amax)[1] - 1 + 127 - 7
    else:
        mant, ex = np.frexp(amax / 6.0)
        byte = np.where(mant > 0.5, ex, ex - 1) + 127
    byte = np.clip(np.where(amax > 0, byte, 1), 1, 254)
    scaled = (w * np.exp2(127.0 - byte)[:, None, :]).reshape(k, n).astype(np.float32)
    by_word = np.ascontiguousarray(scaled.reshape(k // 512, 128, 4, n).transpose(0, 1, 3, 2))
    if fmt == "e4m3":
        words = by_word.astype(ml_dtypes.float8_e4m3fn).view(np.uint8)
    else:
        c = by_word.astype(ml_dtypes.float4_e2m1fn).view(np.uint8) & 0xF
        words = (c[..., 0::2] | (c[..., 1::2] << 4)).reshape(k // 512, 128, 2 * n)
    return np.ascontiguousarray(words), np.ascontiguousarray(byte.astype(np.uint8).reshape(k // 512, 16, n))


def unpack_weight(words, scales, fmt):
    g, _, n = scales.shape
    words = np.ascontiguousarray(words).reshape(g, 128, n, -1)
    if fmt == "e4m3":
        vals = words.view(ml_dtypes.float8_e4m3fn).astype(np.float64)
    else:
        nib = np.empty((g, 128, n, 4), np.uint8)
        nib[..., 0::2] = words & 0xF
        nib[..., 1::2] = words >> 4
        vals = E2M1[nib]
    vals = vals * np.repeat(np.exp2(scales.astype(np.float64) - 127.0), 8, axis=1)[..., None]
    return vals.transpose(0, 1, 3, 2).reshape(g * 512, n)


def gelu(v):
    return 0.5 * v * (1.0 + np.tanh(np.sqrt(2.0 / np.pi) * (v + 0.044715 * v**3)))


K, K2, H, N, T, S, T2, P = 1024, 512, 1024, 512, 2048, 512, 2048, 1024

def setup_inputs():
    n = np.random.standard_normal
    s, s2, u = mx_kscale(K)[:, None], mx_kscale(K2)[:, None], mx_kscale(H)[:, None]
    d = {}
    d["tab_words"], d["tab_scales"] = pack_weight(n((K, T)) * s, "e4m3")
    d["offs"] = striped(np.random.permutation(T)[:S])
    d["tab2_words"], d["tab2_scales"] = pack_weight(n((K2, T)) * s2, "e4m3")
    d["offs2"] = striped(np.random.permutation(T)[:S])
    perm = np.random.permutation(T2)
    d["offs3"] = striped(perm[:S])
    d["offs4"] = striped(perm[S:2 * S])
    d["offs5"] = striped(np.random.permutation(T2)[:P])
    d["w1"] = (1.3 * n((K, H)) / K**0.5 / s).astype(np.float32)
    d["gain"] = (1.3 * np.exp(0.3 * n(H)) * u[:, 0]).astype(np.float32)
    d["w2_words"], d["w2_scales"] = pack_weight(n((K2, H)) / K2**0.5 / s2 * u.T, "e2m1")
    d["wg1"] = np.exp(0.3 * n((128, S))).astype(np.float32)
    d["wg2"] = np.exp(0.3 * n((128, S))).astype(np.float32)
    d["page0"] = (n((H, T2)) * u).astype(np.float32)
    d["bias"] = (0.7 * n(H) * u[:, 0]).astype(np.float32)
    d["w3"] = (n((H, N)) / H**0.5 / u).astype(np.float32)
    return d

def reference(tab_words, tab_scales, offs, tab2_words, tab2_scales, offs2, offs3, offs4, offs5,
              w1, gain, w2_words, w2_scales, wg1, wg2, page0, bias, w3):
    v = unpack_weight(tab_words, tab_scales, "e4m3")[:, unstriped(offs)]
    v2 = unpack_weight(tab2_words, tab2_scales, "e4m3")[:, unstriped(offs2)]
    w2 = unpack_weight(w2_words, w2_scales, "e2m1")
    h1 = f64(gain)[:, None] * np.tanh(mxq(f64(w1), 0, "e4m3").T @ v)
    h2 = np.abs(w2.T @ v2)
    page = f64(page0).copy()
    page[:, unstriped(offs3)] = np.tile(f64(wg1), (H // 128, 1)) * h1
    page[:, unstriped(offs4)] = np.tile(f64(wg2), (H // 128, 1)) * h2
    x = page[:, unstriped(offs5)] + f64(bias)[:, None]
    out = mxq(f64(w3), 0, "e4m3").T @ mxq(x, 0, "e4m3")
    return out

@@ -1,0 +1,374 @@
+from contextlib import ExitStack
+
+import concourse.mybir as mybir
+from concourse.masks import make_identity
+
+K, K2, H, N, T, S, T2, R = 1024, 512, 1024, 512, 2048, 512, 2048, 1024
+FLOPS = 2 * (K * H * S + K2 * H * S + H * N * R)
+
+F32 = mybir.dt.float32
+BF16 = mybir.dt.bfloat16
+I32 = mybir.dt.int32
+U32 = mybir.dt.uint32
+U16 = mybir.dt.uint16
+U8 = mybir.dt.uint8
+FP8X4 = mybir.dt.float8_e4m3fn_x4
+FP4X4 = mybir.dt.float4_e2m1fn_x4
+ACT = mybir.ActivationFunctionType
+MULT = mybir.AluOpType.mult
+
+P = 128
+PACK = 4
+PASS = P * PACK
+SLICES = H // P
+CHUNK = 256
+CHUNKS = R // CHUNK
+ALIGN = 64
+
+
+def tile_list_sleep_night_page_kernel(
+    tc, tab_words, tab_scales, offs, tab2_words, tab2_scales, offs2, offs3, offs4, offs5,
+    w1, gain, w2_words, w2_scales, wg1, wg2, page0, bias, w3, out,
+):
+    nc = tc.nc
+    with ExitStack() as ctx:
+        lists = ctx.enter_context(tc.tile_pool(name="lists", bufs=1))
+        sb = ctx.enter_context(tc.tile_pool(name="sb", bufs=1))
+        ps = ctx.enter_context(tc.psum_pool(name="ps", bufs=1))
+
+        def sbuf(shape, dtype, name, tag=None):
+            return sb.tile(shape, dtype, name=name, tag=tag or name, align_bytes=ALIGN)
+
+        def bank(k, name):
+            return ps.tile([P, 512], F32, name=name, tag="bank%d" % k)
+
+        def load_list(src, name):
+            dst = lists.tile([P, src.shape[1]], U16, name=name, tag=name)
+            nc.sync.dma_start(dst[:], src)
+            return dst
+
+        def zeroed_plane(width, name, engine):
+            plane = sbuf([P, width], U8, name)
+            engine.memset(plane[:].bitcast(I32), 0)
+            return plane
+
+        def load_plane(plane, scales, queue):
+            rows = 4 * scales.shape[0]
+            for q in range(4):
+                queue.dma_start(
+                    plane[32 * q : 32 * q + rows, :].bitcast(I32),
+                    scales[:, 4 * q : 4 * q + 4, :].bitcast(I32),
+                )
+
+        def load_words(words, name):
+            dst = sbuf([P, T], I32, name)
+            nc.sync.dma_start(dst[:], words.rearrange("p t i -> p (t i)").bitcast(I32))
+            return dst
+
+        def load_page(s):
+            b, t = divmod(s, PACK)
+            dst = sbuf([P, T2], F32, "page%d" % s)
+            nc.sync.dma_start(dst[:], page0[b * PASS + t : (b + 1) * PASS : PACK, :])
+            return dst
+
+        def load_weight(w, a, cols, name, tag):
+            raw = sbuf([P, PACK, PASS], F32, name, tag)
+            rows = w[a * PASS : (a + 1) * PASS, cols]
+            nc.sync.dma_start(raw[:], rows.rearrange("(p j) c -> p j c", j=PACK))
+            return raw
+
+        def load_rows(src, name):
+            dst = sbuf([P, S], F32, name)
+            nc.sync.dma_start(dst[:], src)
+            return dst
+
+        def load_channels(vec, name):
+            dst = sbuf([P, H // PASS, PACK], F32, name)
+            nc.sync.dma_start(dst[:], vec.rearrange("(b p t) -> p b t", p=P, t=PACK))
+            return dst
+
+        def deal_factor(raw, name, tag):
+            turned = bank(0, name + "_turned")
+            for c in range(S // P):
+                nc.tensor.transpose(turned[:, c * P : (c + 1) * P], raw[:, c * P : (c + 1) * P], ident[:])
+            spread = sbuf([P, PACK, S // P, P], F32, name + "_spread", tag)
+            return turned, spread
+
+        def deal_slot(turned, spread, t, name):
+            by_t = turned[:].rearrange("p (c m t) -> p t c m", c=S // P, t=PACK)
+            nc.scalar.activation(
+                spread[:, t].rearrange("p c (a m) -> p c a m", a=4),
+                by_t[:, t].unsqueeze(2).broadcast_to([P, S // P, 4, 32]),
+                ACT.Copy,
+            )
+            back = bank(1 + t, name + "_back")
+            for c in range(S // P):
+                nc.tensor.transpose(back[:, c * P : (c + 1) * P], spread[:, t, c, :], ident[:])
+            dealt = sbuf([P, S], F32, name)
+            nc.scalar.copy(dealt[:], back[:])
+            return dealt
+
+        def gather_words(table, offsets, name):
+            dst = sbuf([P, S], U32, name)
+            nc.vector.tensor_copy(dst[:], table[:].bitcast(U32).indirect(offsets[:]))
+            return dst
+
+        def gather_plane(plane, offsets, name):
+            dst = sbuf([P, S], U8, name)
+            nc.vector.tensor_copy(dst[:], plane[:].indirect(offsets[:]))
+            return dst
+
+        def quantise(grouped, name, tag=None):
+            width = grouped.shape[1] // PACK
+            codes = sbuf([P, width], U32, name + "_codes", tag)
+            plane = sbuf([P, width], U8, name + "_plane")
+            nc.vector.quantize_mx(out=codes[:].bitcast(FP8X4), scales=plane[:], in_=grouped[:])
+            return codes, plane
+
+        def quantise_w1(raw, name, tag):
+            grouped = sbuf([P, PACK * PASS], BF16, name + "_grouped", tag)
+            nc.scalar.copy(
+                grouped[:].rearrange("p (t m j) -> p m t j", t=PACK, j=PACK),
+                raw[:].rearrange("p j (m t) -> p m t j", t=PACK),
+            )
+            return quantise(grouped, name)
+
+        def quantise_w3(raw, name, tag):
+            grouped = sbuf([P, PACK * N], BF16, name + "_grouped", tag)
+            nc.scalar.copy(
+                grouped[:].rearrange("p (c i j) -> p c j i", i=4, j=PACK),
+                raw[:].rearrange("p j (c i) -> p c j i", i=4),
+            )
+            return quantise(grouped, name)
+
+        def airflow_features(s):
+            acc = bank(5 + s % 3, "acc2_%d" % s)
+            nc.tensor.matmul_mx(
+                out=acc[:],
+                lhsT=w2_codes[:, 2 * s * P : 2 * (s + 1) * P].bitcast(FP4X4),
+                lhsT_scale=w2_plane[:, s * P : (s + 1) * P],
+                rhs=v2_codes[:].bitcast(FP8X4),
+                rhs_scale=v2_plane[:],
+                start=True,
+                stop=True,
+            )
+            h2 = sbuf([P, S], F32, "h2_%d" % s, "row%d" % s)
+            nc.scalar.activation(h2[:], acc[:], ACT.Abs)
+            return h2
+
+        def eeg_bounded(s, w1_q):
+            t = s % PACK
+            acc = bank(5 + s % 3, "acc1_%d" % s)
+            for a in range(K // PASS):
+                codes, plane = w1_q[a]
+                nc.tensor.matmul_mx(
+                    out=acc[:],
+                    lhsT=codes[:, t * P : (t + 1) * P].bitcast(FP8X4),
+                    lhsT_scale=plane[:, t * P : (t + 1) * P],
+                    rhs=v_codes[a][:].bitcast(FP8X4),
+                    rhs_scale=v_plane[4 * a : P, :],
+                    start=(a == 0),
+                    stop=(a == K // PASS - 1),
+                )
+            bounded = sbuf([P, S], F32, "bounded%d" % s, "bounded%d" % (s % 2))
+            nc.scalar.activation(bounded[:], acc[:], ACT.Tanh)
+            return bounded
+
+        def eeg_features(s, bounded, tag):
+            b, t = divmod(s, PACK)
+            h1 = sbuf([P, S], F32, "h1_%d" % s, tag)
+            nc.scalar.activation(h1[:], bounded[:], ACT.Copy, scale=gains[:, b, t : t + 1])
+            return h1
+
+        def put(s, offsets, h, factor):
+            nc.vector.tensor_tensor(pages[s][:].indirect(offsets[:]), h[:], factor[s % PACK][:], MULT)
+
+        def fetch(s, tag):
+            picked = sbuf([P, R], F32, "picked%d" % s, tag)
+            nc.vector.tensor_copy(picked[:], pages[s][:].indirect(read_list[:]))
+            return picked
+
+        def add_bias(s, picked, grouped):
+            b, t = divmod(s, PACK)
+            nc.scalar.activation(
+                grouped.rearrange("p (n t) -> p n t", t=PACK)[:, :, t],
+                picked,
+                ACT.Identity,
+                bias=biases[:, b, t : t + 1],
+            )
+
+        def score(acc, half, a, codes, plane):
+            w_codes, w_plane = w3_q[a]
+            for i in range(2):
+                n = 2 * half + i
+                nc.tensor.matmul_mx(
+                    out=acc[:, i * CHUNK : (i + 1) * CHUNK],
+                    lhsT=w_codes[:, n * P : (n + 1) * P].bitcast(FP8X4),
+                    lhsT_scale=w_plane[:, n * P : (n + 1) * P],
+                    rhs=codes.bitcast(FP8X4),
+                    rhs_scale=plane,
+                    start=(a == 0 and i == 0),
+                    stop=(a == 1 and i == 1),
+                )
+
+        v2_window = zeroed_plane(T, "v2_window", nc.gpsimd)
+        w2_raw_plane = zeroed_plane(H, "w2_raw_plane", nc.vector)
+        v_window = zeroed_plane(T, "v_window", nc.vector)
+
+        pages = [None] * SLICES
+        low, high = slice(0, PASS), slice(PASS, H)
+        w2_raw = sbuf([P, 2 * H], U8, "w2_raw")
+        nc.sync.dma_start(w2_raw[:].bitcast(I32), w2_words[0].bitcast(I32))
+        wg2_raw = load_rows(wg2, "wg2_raw")
+        load_plane(v2_window, tab2_scales, nc.sync)
+        air_list = load_list(offs2, "air_list")
+        v2_table = load_words(tab2_words[0], "v2_table")
+        load_plane(w2_raw_plane, w2_scales, nc.sync)
+        air_slots = load_list(offs4, "air_slots")
+        pages[0] = load_page(0)
+        pages[1] = load_page(1)
+        eeg_list = load_list(offs, "eeg_list")
+        load_plane(v_window, tab_scales, nc.sync)
+        v_table = [load_words(tab_words[0], "v_table0")]
+        pages[2] = load_page(2)
+        w1_raw = {(0, 0): load_weight(w1, 0, low, "w1_raw00", "raw0")}
+        pages[3] = load_page(3)
+        wg1_raw = load_rows(wg1, "wg1_raw")
+        gains = load_channels(gain, "gains")
+        w1_raw[1, 0] = load_weight(w1, 1, low, "w1_raw10", "raw1")
+        eeg_slots = load_list(offs3, "eeg_slots")
+        pages[4] = load_page(4)
+        read_list = load_list(offs5, "read_list")
+        v_table.append(load_words(tab_words[1], "v_table1"))
+        biases = load_channels(bias, "biases")
+        pages[5] = load_page(5)
+
+        ident = sbuf([P, P], F32, "ident")
+        make_identity(nc, ident[:])
+        turned, spread = deal_factor(wg2_raw, "wg2", "raw2")
+        w2_codes = sbuf([P, 2 * H], U8, "w2_codes")
+        nc.vector.tensor_copy(
+            w2_codes[:].bitcast(U16).rearrange("p (b t m) -> p b t m", t=PACK, m=P),
+            w2_raw[:].bitcast(U16).rearrange("p (b m t) -> p b t m", t=PACK, m=P),
+        )
+        v2_plane = gather_plane(v2_window, air_list, "v2_plane")
+        v2_codes = gather_words(v2_table, air_list, "v2_codes")
+        w2_plane = sbuf([P, H], U8, "w2_plane")
+        nc.vector.tensor_copy(
+            w2_plane[:].rearrange("p (b t m) -> p b t m", t=PACK, m=P),
+            w2_raw_plane[:].rearrange("p (b m t) -> p b t m", t=PACK, m=P),
+        )
+        factor2, h2 = [], []
+        for s in range(SLICES):
+            if s < PACK:
+                factor2.append(deal_slot(turned, spread, s, "factor2_%d" % s))
+            h2.append(airflow_features(s))
+
+        w1_raw[0, 1] = load_weight(w1, 0, high, "w1_raw01", "raw2")
+        w1_raw[1, 1] = load_weight(w1, 1, high, "w1_raw11", "raw3")
+
+        put(0, air_slots, h2[0], factor2)
+        put(1, air_slots, h2[1], factor2)
+        v_plane = gather_plane(v_window, eeg_list, "v_plane")
+        v_codes = [gather_words(v_table[0], eeg_list, "v_codes0")]
+        put(2, air_slots, h2[2], factor2)
+        w1_low = [quantise_w1(w1_raw[0, 0], "w1_00", "grouped0")]
+        turned, spread = deal_factor(wg1_raw, "wg1", "v2_table")
+        factor1 = [deal_slot(turned, spread, t, "factor1_%d" % t) for t in range(PACK)]
+        put(3, air_slots, h2[3], factor2)
+
+        w3_raw = [load_weight(w3, 0, slice(0, N), "w3_raw0", "raw0")]
+        pages[6] = load_page(6)
+
+        put(4, air_slots, h2[4], factor2)
+        w1_low.append(quantise_w1(w1_raw[1, 0], "w1_10", "grouped1"))
+
+        w3_raw.append(load_weight(w3, 1, slice(0, N), "w3_raw1", "raw1"))
+        pages[7] = load_page(7)
+
+        v_codes.append(gather_words(v_table[1], eeg_list, "v_codes1"))
+        h1 = [eeg_features(s, eeg_bounded(s, w1_low), "row%d" % s) for s in range(3)]
+        bounded = eeg_bounded(3, w1_low)
+        put(5, air_slots, h2[5], factor2)
+        for s in range(3):
+            put(s, eeg_slots, h1[s], factor1)
+        w1_high = [
+            quantise_w1(w1_raw[a, 1], "w1_%d1" % a, "grouped%d" % a) for a in range(K // PASS)
+        ]
+        h1.append(eeg_features(3, bounded, "grouped0"))
+        picked = {0: fetch(0, "grouped1")}
+        w3_q = [quantise_w3(w3_raw[a], "w3_%d" % a, "v_table%d" % a) for a in range(H // PASS)]
+        h1.extend([eeg_features(s, eeg_bounded(s, w1_high), "row%d" % (s % 5)) for s in range(4, 7)])
+        bounded = eeg_bounded(7, w1_high)
+        put(3, eeg_slots, h1[3], factor1)
+        picked[1] = fetch(1, "grouped0")
+        put(6, air_slots, h2[6], factor2)
+
+        low_cuts = [(0, CHUNK, "raw1"), (CHUNK, 2 * CHUNK, "raw0"), (2 * CHUNK, R, "raw2")]
+        x_low = [sbuf([P, PACK * (hi - lo)], BF16, "x_low%d" % lo, tag) for lo, hi, tag in low_cuts]
+        x_high = [sbuf([P, PACK * CHUNK], BF16, "x_high%d" % c) for c in range(CHUNKS)]
+
+        def bias_low(s):
+            for (lo, hi, tag), grouped in zip(low_cuts, x_low):
+                add_bias(s, picked[s][:, lo:hi], grouped[:])
+
+        def score_low(u, tag):
+            lo, hi = low_cuts[u][:2]
+            codes, plane = quantise(x_low[u], "x_low%d" % lo, tag)
+            for c in range(lo // CHUNK, hi // CHUNK):
+                cols = slice(c * CHUNK - lo, (c + 1) * CHUNK - lo)
+                for half in range(2):
+                    accs[c, half] = bank(2 * c + half, "score%d_%d" % (c, half))
+                    score(accs[c, half], half, 0, codes[:, cols], plane[:, cols])
+
+        def bias_high(s):
+            for c in range(CHUNKS):
+                add_bias(s, picked[s][:, c * CHUNK : (c + 1) * CHUNK], x_high[c][:])
+
+        bias_low(0)
+        bias_low(1)
+        put(4, eeg_slots, h1[4], factor1)
+        picked[2] = fetch(2, "row4")
+        bias_low(2)
+        put(5, eeg_slots, h1[5], factor1)
+        picked[3] = fetch(3, "row0")
+        bias_low(3)
+        put(6, eeg_slots, h1[6], factor1)
+        picked[4] = fetch(4, "row1")
+        bias_high(4)
+        put(7, air_slots, h2[7], factor2)
+        accs = {}
+        score_low(0, "raw3")
+        score_low(1, "v2_table")
+        picked[5] = fetch(5, "raw1")
+        h1.append(eeg_features(7, bounded, "page5"))
+        bias_high(5)
+        picked[6] = fetch(6, "raw0")
+        bias_high(6)
+        put(7, eeg_slots, h1[7], factor1)
+        score_low(2, "page5")
+
+        last = SLICES - 1
+        picked_last = sbuf([P, R], F32, "picked_last", "row5")
+        for c in range(CHUNKS):
+            cols = slice(c * CHUNK, (c + 1) * CHUNK)
+            part = read_list[:, c * CHUNK // 16 : (c + 1) * CHUNK // 16]
+            nc.vector.tensor_copy(picked_last[:, cols], pages[last][:].indirect(part))
+            add_bias(last, picked_last[:, cols], x_high[c][:])
+        out_rows = out.rearrange("(n p) j -> p n j", p=P)
+        for c in range(CHUNKS):
+            cols = slice(c * CHUNK, (c + 1) * CHUNK)
+            codes, plane = quantise(x_high[c], "x_high%d" % c)
+            for half in range(2):
+                score(accs[c, half], half, 1, codes[:], plane[:])
+            for half in range(2):
+                tag = ("page%d" % c, "row%d" % (c + 1))[half]
+                staged = sbuf([P, 2 * CHUNK], F32, "staged%d_%d" % (c, half), tag)
+                if half == 1:
+                    nc.scalar.copy(staged[:], accs[c, half][:])
+                else:
+                    nc.vector.tensor_copy(staged[:], accs[c, half][:])
+                nc.sync.dma_start(
+                    out_rows[:, 2 * half : 2 * half + 2, cols],
+                    staged[:].rearrange("p (i j) -> p i j", i=2),
+                )

@@ -21,9 +21,11 @@ P = 128
 PACK = 4
 PASS = P * PACK
 SLICES = H // P
-CHUNK = 256
-CHUNKS = R // CHUNK
+CUTS = (0, 256, 512, 768, 1024)
+CHUNKS = len(CUTS) - 1
+BANK = 512
 ALIGN = 64
+STAGE_TAGS = ("page0", "page1", "page2", "page3", "page4", "page6", "row6", "row7")
 
 
 def tile_list_sleep_night_page_kernel(
@@ -94,27 +96,27 @@ def tile_list_sleep_night_page_kernel(
             spread = sbuf([P, PACK, S // P, P], F32, name + "_spread", tag)
             return turned, spread
 
-        def deal_slot(turned, spread, t, name):
+        def deal_slot(turned, spread, t, name, which):
             by_t = turned[:].rearrange("p (c m t) -> p t c m", c=S // P, t=PACK)
             nc.scalar.activation(
                 spread[:, t].rearrange("p c (a m) -> p c a m", a=4),
                 by_t[:, t].unsqueeze(2).broadcast_to([P, S // P, 4, 32]),
                 ACT.Copy,
             )
-            back = bank(1 + t, name + "_back")
+            back = bank(which, name + "_back")
             for c in range(S // P):
                 nc.tensor.transpose(back[:, c * P : (c + 1) * P], spread[:, t, c, :], ident[:])
             dealt = sbuf([P, S], F32, name)
             nc.scalar.copy(dealt[:], back[:])
             return dealt
 
-        def gather_words(table, offsets, name):
-            dst = sbuf([P, S], U32, name)
+        def gather_words(table, offsets, name, tag=None):
+            dst = sbuf([P, S], U32, name, tag)
             nc.vector.tensor_copy(dst[:], table[:].bitcast(U32).indirect(offsets[:]))
             return dst
 
-        def gather_plane(plane, offsets, name):
-            dst = sbuf([P, S], U8, name)
+        def gather_plane(plane, offsets, name, tag=None):
+            dst = sbuf([P, S], U8, name, tag)
             nc.vector.tensor_copy(dst[:], plane[:].indirect(offsets[:]))
             return dst
 
@@ -146,7 +148,7 @@ def tile_list_sleep_night_page_kernel(
             nc.tensor.matmul_mx(
                 out=acc[:],
                 lhsT=w2_codes[:, 2 * s * P : 2 * (s + 1) * P].bitcast(FP4X4),
-                lhsT_scale=w2_plane[:, s * P : (s + 1) * P],
+                lhsT_scale=w2_plane[s % PACK][:, s // PACK, :],
                 rhs=v2_codes[:].bitcast(FP8X4),
                 rhs_scale=v2_plane[:],
                 start=True,
@@ -197,23 +199,30 @@ def tile_list_sleep_night_page_kernel(
                 bias=biases[:, b, t : t + 1],
             )
 
-        def score(acc, half, a, codes, plane):
+        def score(c, a, codes, plane):
             w_codes, w_plane = w3_q[a]
-            for i in range(2):
-                n = 2 * half + i
+            width = CUTS[c + 1] - CUTS[c]
+            per_bank = BANK // width
+            for n in range(N // P):
+                k, i = divmod(n, per_bank)
+                if a == 0 and i == 0:
+                    accs[c].append(bank(CUTS[c] // P + k, "score%d_%d" % (c, k)))
                 nc.tensor.matmul_mx(
-                    out=acc[:, i * CHUNK : (i + 1) * CHUNK],
+                    out=accs[c][k][:, i * width : (i + 1) * width],
                     lhsT=w_codes[:, n * P : (n + 1) * P].bitcast(FP8X4),
                     lhsT_scale=w_plane[:, n * P : (n + 1) * P],
                     rhs=codes.bitcast(FP8X4),
                     rhs_scale=plane,
                     start=(a == 0 and i == 0),
-                    stop=(a == 1 and i == 1),
+                    stop=(a == 1 and i == per_bank - 1),
                 )
 
         v2_window = zeroed_plane(T, "v2_window", nc.gpsimd)
         w2_raw_plane = zeroed_plane(H, "w2_raw_plane", nc.vector)
-        v_window = zeroed_plane(T, "v_window", nc.vector)
+
+        ident = sbuf([P, P], F32, "ident")
+        make_identity(nc, ident[:])
+        v_window = zeroed_plane(T, "v_window", nc.gpsimd)
 
         pages = [None] * SLICES
         low, high = slice(0, PASS), slice(PASS, H)
@@ -233,18 +242,16 @@ def tile_list_sleep_night_page_kernel(
         pages[2] = load_page(2)
         w1_raw = {(0, 0): load_weight(w1, 0, low, "w1_raw00", "raw0")}
         pages[3] = load_page(3)
+        w1_raw[1, 0] = load_weight(w1, 1, low, "w1_raw10", "raw1")
         wg1_raw = load_rows(wg1, "wg1_raw")
         gains = load_channels(gain, "gains")
-        w1_raw[1, 0] = load_weight(w1, 1, low, "w1_raw10", "raw1")
+        v_table.append(load_words(tab_words[1], "v_table1"))
         eeg_slots = load_list(offs3, "eeg_slots")
         pages[4] = load_page(4)
         read_list = load_list(offs5, "read_list")
-        v_table.append(load_words(tab_words[1], "v_table1"))
         biases = load_channels(bias, "biases")
         pages[5] = load_page(5)
 
-        ident = sbuf([P, P], F32, "ident")
-        make_identity(nc, ident[:])
         turned, spread = deal_factor(wg2_raw, "wg2", "raw2")
         w2_codes = sbuf([P, 2 * H], U8, "w2_codes")
         nc.vector.tensor_copy(
@@ -253,15 +260,14 @@ def tile_list_sleep_night_page_kernel(
         )
         v2_plane = gather_plane(v2_window, air_list, "v2_plane")
         v2_codes = gather_words(v2_table, air_list, "v2_codes")
-        w2_plane = sbuf([P, H], U8, "w2_plane")
-        nc.vector.tensor_copy(
-            w2_plane[:].rearrange("p (b t m) -> p b t m", t=PACK, m=P),
-            w2_raw_plane[:].rearrange("p (b m t) -> p b t m", t=PACK, m=P),
-        )
+        by_slot = w2_raw_plane[:].rearrange("p (b m t) -> p b t m", t=PACK, m=P)
+        w2_plane = [sbuf([P, H // PASS, P], U8, "w2_plane%d" % t) for t in range(PACK)]
+        for t in range(PACK):
+            nc.vector.tensor_copy(w2_plane[t][:], by_slot[:, :, t, :])
         factor2, h2 = [], []
         for s in range(SLICES):
             if s < PACK:
-                factor2.append(deal_slot(turned, spread, s, "factor2_%d" % s))
+                factor2.append(deal_slot(turned, spread, s, "factor2_%d" % s, 4 + s))
             h2.append(airflow_features(s))
 
         w1_raw[0, 1] = load_weight(w1, 0, high, "w1_raw01", "raw2")
@@ -269,26 +275,24 @@ def tile_list_sleep_night_page_kernel(
 
         put(0, air_slots, h2[0], factor2)
         put(1, air_slots, h2[1], factor2)
-        v_plane = gather_plane(v_window, eeg_list, "v_plane")
-        v_codes = [gather_words(v_table[0], eeg_list, "v_codes0")]
+        v_plane = gather_plane(v_window, eeg_list, "v_plane", "row0")
+        v_codes = [gather_words(v_table[0], eeg_list, "v_codes0", "row1")]
         put(2, air_slots, h2[2], factor2)
         w1_low = [quantise_w1(w1_raw[0, 0], "w1_00", "grouped0")]
-        turned, spread = deal_factor(wg1_raw, "wg1", "v2_table")
-        factor1 = [deal_slot(turned, spread, t, "factor1_%d" % t) for t in range(PACK)]
         put(3, air_slots, h2[3], factor2)
+        w1_low.append(quantise_w1(w1_raw[1, 0], "w1_10", "grouped1"))
+        turned, spread = deal_factor(wg1_raw, "wg1", "v2_table")
+        factor1 = [deal_slot(turned, spread, t, "factor1_%d" % t, 1 + t) for t in range(PACK)]
 
         w3_raw = [load_weight(w3, 0, slice(0, N), "w3_raw0", "raw0")]
         pages[6] = load_page(6)
-
-        put(4, air_slots, h2[4], factor2)
-        w1_low.append(quantise_w1(w1_raw[1, 0], "w1_10", "grouped1"))
-
         w3_raw.append(load_weight(w3, 1, slice(0, N), "w3_raw1", "raw1"))
         pages[7] = load_page(7)
 
-        v_codes.append(gather_words(v_table[1], eeg_list, "v_codes1"))
-        h1 = [eeg_features(s, eeg_bounded(s, w1_low), "row%d" % s) for s in range(3)]
+        v_codes.append(gather_words(v_table[1], eeg_list, "v_codes1", "row2"))
+        h1 = [eeg_features(s, eeg_bounded(s, w1_low), ("spare0", "row3", "spare1")[s]) for s in range(3)]
         bounded = eeg_bounded(3, w1_low)
+        put(4, air_slots, h2[4], factor2)
         put(5, air_slots, h2[5], factor2)
         for s in range(3):
             put(s, eeg_slots, h1[s], factor1)
@@ -298,46 +302,48 @@ def tile_list_sleep_night_page_kernel(
         h1.append(eeg_features(3, bounded, "grouped0"))
         picked = {0: fetch(0, "grouped1")}
         w3_q = [quantise_w3(w3_raw[a], "w3_%d" % a, "v_table%d" % a) for a in range(H // PASS)]
-        h1.extend([eeg_features(s, eeg_bounded(s, w1_high), "row%d" % (s % 5)) for s in range(4, 7)])
+        h1.extend([eeg_features(s, eeg_bounded(s, w1_high), ("row4", "row5", "row1")[s - 4]) for s in range(4, 7)])
         bounded = eeg_bounded(7, w1_high)
         put(3, eeg_slots, h1[3], factor1)
-        picked[1] = fetch(1, "grouped0")
+        picked[1] = fetch(1, "page0")
         put(6, air_slots, h2[6], factor2)
 
-        low_cuts = [(0, CHUNK, "raw1"), (CHUNK, 2 * CHUNK, "raw0"), (2 * CHUNK, R, "raw2")]
-        x_low = [sbuf([P, PACK * (hi - lo)], BF16, "x_low%d" % lo, tag) for lo, hi, tag in low_cuts]
-        x_high = [sbuf([P, PACK * CHUNK], BF16, "x_high%d" % c) for c in range(CHUNKS)]
+        low_parts = [((0,), "raw1"), ((1,), "raw0"), ((2, 3), "raw2")]
+        low_cuts = [(CUTS[part[0]], CUTS[part[-1] + 1]) for part, tag in low_parts]
+        x_low = [
+            sbuf([P, PACK * (hi - lo)], BF16, "x_low%d" % lo, tag)
+            for (lo, hi), (part, tag) in zip(low_cuts, low_parts)
+        ]
+        x_high = [sbuf([P, PACK * (CUTS[c + 1] - CUTS[c])], BF16, "x_high%d" % c) for c in range(CHUNKS)]
+        accs = [[] for c in range(CHUNKS)]
 
         def bias_low(s):
-            for (lo, hi, tag), grouped in zip(low_cuts, x_low):
+            for (lo, hi), grouped in zip(low_cuts, x_low):
                 add_bias(s, picked[s][:, lo:hi], grouped[:])
 
         def score_low(u, tag):
-            lo, hi = low_cuts[u][:2]
+            lo = low_cuts[u][0]
             codes, plane = quantise(x_low[u], "x_low%d" % lo, tag)
-            for c in range(lo // CHUNK, hi // CHUNK):
-                cols = slice(c * CHUNK - lo, (c + 1) * CHUNK - lo)
-                for half in range(2):
-                    accs[c, half] = bank(2 * c + half, "score%d_%d" % (c, half))
-                    score(accs[c, half], half, 0, codes[:, cols], plane[:, cols])
+            for c in low_parts[u][0]:
+                cols = slice(CUTS[c] - lo, CUTS[c + 1] - lo)
+                score(c, 0, codes[:, cols], plane[:, cols])
 
         def bias_high(s):
             for c in range(CHUNKS):
-                add_bias(s, picked[s][:, c * CHUNK : (c + 1) * CHUNK], x_high[c][:])
+                add_bias(s, picked[s][:, CUTS[c] : CUTS[c + 1]], x_high[c][:])
 
         bias_low(0)
         bias_low(1)
         put(4, eeg_slots, h1[4], factor1)
-        picked[2] = fetch(2, "row4")
+        picked[2] = fetch(2, "page1")
         bias_low(2)
         put(5, eeg_slots, h1[5], factor1)
-        picked[3] = fetch(3, "row0")
+        picked[3] = fetch(3, "page2")
         bias_low(3)
         put(6, eeg_slots, h1[6], factor1)
-        picked[4] = fetch(4, "row1")
+        picked[4] = fetch(4, "page3")
         bias_high(4)
         put(7, air_slots, h2[7], factor2)
-        accs = {}
         score_low(0, "raw3")
         score_low(1, "v2_table")
         picked[5] = fetch(5, "raw1")
@@ -349,26 +355,34 @@ def tile_list_sleep_night_page_kernel(
         score_low(2, "page5")
 
         last = SLICES - 1
-        picked_last = sbuf([P, R], F32, "picked_last", "row5")
-        for c in range(CHUNKS):
-            cols = slice(c * CHUNK, (c + 1) * CHUNK)
-            part = read_list[:, c * CHUNK // 16 : (c + 1) * CHUNK // 16]
-            nc.vector.tensor_copy(picked_last[:, cols], pages[last][:].indirect(part))
-            add_bias(last, picked_last[:, cols], x_high[c][:])
         out_rows = out.rearrange("(n p) j -> p n j", p=P)
-        for c in range(CHUNKS):
-            cols = slice(c * CHUNK, (c + 1) * CHUNK)
+
+        def fetch_last(c, tag):
+            got = sbuf([P, CUTS[c + 1] - CUTS[c]], F32, "picked_last%d" % c, tag)
+            part = read_list[:, CUTS[c] // 16 : CUTS[c + 1] // 16]
+            nc.vector.tensor_copy(got[:], pages[last][:].indirect(part))
+            add_bias(last, got[:], x_high[c][:])
+
+        def score_high(c):
             codes, plane = quantise(x_high[c], "x_high%d" % c)
-            for half in range(2):
-                score(accs[c, half], half, 1, codes[:], plane[:])
-            for half in range(2):
-                tag = ("page%d" % c, "row%d" % (c + 1))[half]
-                staged = sbuf([P, 2 * CHUNK], F32, "staged%d_%d" % (c, half), tag)
-                if half == 1:
-                    nc.scalar.copy(staged[:], accs[c, half][:])
+            score(c, 1, codes[:], plane[:])
+
+        def store(c):
+            per_bank = (N // P) // len(accs[c])
+            for k, acc in enumerate(accs[c]):
+                which = CUTS[c] // P + k
+                staged = sbuf([P, BANK], F32, "staged%d" % which, STAGE_TAGS[which])
+                if which % 2 == 1:
+                    nc.scalar.copy(staged[:], acc[:])
                 else:
-                    nc.vector.tensor_copy(staged[:], accs[c, half][:])
+                    nc.vector.tensor_copy(staged[:], acc[:])
                 nc.sync.dma_start(
-                    out_rows[:, 2 * half : 2 * half + 2, cols],
-                    staged[:].rearrange("p (i j) -> p i j", i=2),
+                    out_rows[:, k * per_bank : (k + 1) * per_bank, CUTS[c] : CUTS[c + 1]],
+                    staged[:].rearrange("p (i j) -> p i j", i=per_bank),
                 )
+
+        for c in range(CHUNKS):
+            fetch_last(c, "picked_last%d" % c)
+        for c in range(CHUNKS):
+            score_high(c)
+            store(c)

@@ -290,23 +290,21 @@ def tile_list_sleep_night_page_kernel(
         pages[7] = load_page(7)
 
         v_codes.append(gather_words(v_table[1], eeg_list, "v_codes1", "row2"))
-        h1 = [eeg_features(s, eeg_bounded(s, w1_low), ("spare0", "row3", "spare1")[s]) for s in range(3)]
-        bounded = eeg_bounded(3, w1_low)
+        low_tags = ("spare0", "row3", "spare1", "spare2")
+        h1 = [eeg_features(s, eeg_bounded(s, w1_low), low_tags[s]) for s in range(PACK)]
         put(4, air_slots, h2[4], factor2)
         put(5, air_slots, h2[5], factor2)
-        for s in range(3):
+        for s in range(PACK):
             put(s, eeg_slots, h1[s], factor1)
         w1_high = [
             quantise_w1(w1_raw[a, 1], "w1_%d1" % a, "grouped%d" % a) for a in range(K // PASS)
         ]
-        h1.append(eeg_features(3, bounded, "grouped0"))
-        picked = {0: fetch(0, "grouped1")}
         w3_q = [quantise_w3(w3_raw[a], "w3_%d" % a, "v_table%d" % a) for a in range(H // PASS)]
+        picked = {0: fetch(0, "grouped1")}
         h1.extend([eeg_features(s, eeg_bounded(s, w1_high), ("row4", "row5", "row1")[s - 4]) for s in range(4, 7)])
         bounded = eeg_bounded(7, w1_high)
-        put(3, eeg_slots, h1[3], factor1)
-        picked[1] = fetch(1, "page0")
         put(6, air_slots, h2[6], factor2)
+        picked[1] = fetch(1, "page0")
 
         low_parts = [((0,), "raw1"), ((1,), "raw0"), ((2, 3), "raw2")]
         low_cuts = [(CUTS[part[0]], CUTS[part[-1] + 1]) for part, tag in low_parts]
@@ -344,15 +342,15 @@ def tile_list_sleep_night_page_kernel(
         picked[4] = fetch(4, "page3")
         bias_high(4)
         put(7, air_slots, h2[7], factor2)
+        picked[5] = fetch(5, "page4")
+        bias_high(5)
         score_low(0, "raw3")
         score_low(1, "v2_table")
-        picked[5] = fetch(5, "raw1")
-        h1.append(eeg_features(7, bounded, "page5"))
-        bias_high(5)
-        picked[6] = fetch(6, "raw0")
+        h1.append(eeg_features(7, bounded, "raw0"))
+        picked[6] = fetch(6, "raw1")
         bias_high(6)
         put(7, eeg_slots, h1[7], factor1)
-        score_low(2, "page5")
+        score_low(2, "raw0")
 
         last = SLICES - 1
         out_rows = out.rearrange("(n p) j -> p n j", p=P)

@@ -233,8 +233,8 @@ def tile_list_sleep_night_page_kernel(
         air_list = load_list(offs2, "air_list")
         v2_table = load_words(tab2_words[0], "v2_table")
         load_plane(w2_raw_plane, w2_scales, nc.sync)
-        air_slots = load_list(offs4, "air_slots")
         pages[0] = load_page(0)
+        air_slots = load_list(offs4, "air_slots")
         pages[1] = load_page(1)
         eeg_list = load_list(offs, "eeg_list")
         load_plane(v_window, tab_scales, nc.sync)
@@ -290,21 +290,23 @@ def tile_list_sleep_night_page_kernel(
         pages[7] = load_page(7)
 
         v_codes.append(gather_words(v_table[1], eeg_list, "v_codes1", "row2"))
-        low_tags = ("spare0", "row3", "spare1", "spare2")
-        h1 = [eeg_features(s, eeg_bounded(s, w1_low), low_tags[s]) for s in range(PACK)]
+        h1 = [eeg_features(s, eeg_bounded(s, w1_low), ("spare0", "row3", "spare1")[s]) for s in range(3)]
+        bounded = eeg_bounded(3, w1_low)
         put(4, air_slots, h2[4], factor2)
         put(5, air_slots, h2[5], factor2)
-        for s in range(PACK):
+        for s in range(3):
             put(s, eeg_slots, h1[s], factor1)
         w1_high = [
             quantise_w1(w1_raw[a, 1], "w1_%d1" % a, "grouped%d" % a) for a in range(K // PASS)
         ]
+        h1.append(eeg_features(3, bounded, "grouped0"))
+        picked = {0: fetch(0, "raw3")}
         w3_q = [quantise_w3(w3_raw[a], "w3_%d" % a, "v_table%d" % a) for a in range(H // PASS)]
-        picked = {0: fetch(0, "grouped1")}
         h1.extend([eeg_features(s, eeg_bounded(s, w1_high), ("row4", "row5", "row1")[s - 4]) for s in range(4, 7)])
         bounded = eeg_bounded(7, w1_high)
-        put(6, air_slots, h2[6], factor2)
+        put(3, eeg_slots, h1[3], factor1)
         picked[1] = fetch(1, "page0")
+        put(6, air_slots, h2[6], factor2)
 
         low_parts = [((0,), "raw1"), ((1,), "raw0"), ((2, 3), "raw2")]
         low_cuts = [(CUTS[part[0]], CUTS[part[-1] + 1]) for part, tag in low_parts]
@@ -342,21 +344,21 @@ def tile_list_sleep_night_page_kernel(
         picked[4] = fetch(4, "page3")
         bias_high(4)
         put(7, air_slots, h2[7], factor2)
-        picked[5] = fetch(5, "page4")
-        bias_high(5)
         score_low(0, "raw3")
         score_low(1, "v2_table")
-        h1.append(eeg_features(7, bounded, "raw0"))
-        picked[6] = fetch(6, "raw1")
+        picked[5] = fetch(5, "page2")
+        h1.append(eeg_features(7, bounded, "page5"))
+        bias_high(5)
+        picked[6] = fetch(6, "page3")
         bias_high(6)
         put(7, eeg_slots, h1[7], factor1)
-        score_low(2, "raw0")
+        score_low(2, "bounded1")
 
         last = SLICES - 1
         out_rows = out.rearrange("(n p) j -> p n j", p=P)
 
         def fetch_last(c, tag):
-            got = sbuf([P, CUTS[c + 1] - CUTS[c]], F32, "picked_last%d" % c, tag)
+            got = sbuf([P, CUTS[c + 1] - CUTS[c]], F32, "picked_last_%d" % c, tag)
             part = read_list[:, CUTS[c] // 16 : CUTS[c + 1] // 16]
             nc.vector.tensor_copy(got[:], pages[last][:].indirect(part))
             add_bias(last, got[:], x_high[c][:])
@@ -379,8 +381,11 @@ def tile_list_sleep_night_page_kernel(
                     staged[:].rearrange("p (i j) -> p i j", i=per_bank),
                 )
 
-        for c in range(CHUNKS):
+        for c in range(CHUNKS - 1):
             fetch_last(c, "picked_last%d" % c)
-        for c in range(CHUNKS):
+        score_high(0)
+        fetch_last(CHUNKS - 1, "picked_last0")
+        store(0)
+        for c in range(1, CHUNKS):
             score_high(c)
             store(c)

@@ -233,11 +233,11 @@ def tile_list_sleep_night_page_kernel(
         air_list = load_list(offs2, "air_list")
         v2_table = load_words(tab2_words[0], "v2_table")
         load_plane(w2_raw_plane, w2_scales, nc.sync)
+        eeg_list = load_list(offs, "eeg_list")
         pages[0] = load_page(0)
         air_slots = load_list(offs4, "air_slots")
         pages[1] = load_page(1)
-        eeg_list = load_list(offs, "eeg_list")
-        load_plane(v_window, tab_scales, nc.sync)
+        load_plane(v_window, tab_scales, nc.gpsimd)
         v_table = [load_words(tab_words[0], "v_table0")]
         pages[2] = load_page(2)
         w1_raw = {(0, 0): load_weight(w1, 0, low, "w1_raw00", "raw0")}
@@ -264,6 +264,7 @@ def tile_list_sleep_night_page_kernel(
         w2_plane = [sbuf([P, H // PASS, P], U8, "w2_plane%d" % t) for t in range(PACK)]
         for t in range(PACK):
             nc.vector.tensor_copy(w2_plane[t][:], by_slot[:, :, t, :])
+        v_plane = gather_plane(v_window, eeg_list, "v_plane")
         factor2, h2 = [], []
         for s in range(SLICES):
             if s < PACK:
@@ -275,7 +276,6 @@ def tile_list_sleep_night_page_kernel(
 
         put(0, air_slots, h2[0], factor2)
         put(1, air_slots, h2[1], factor2)
-        v_plane = gather_plane(v_window, eeg_list, "v_plane", "row0")
         v_codes = [gather_words(v_table[0], eeg_list, "v_codes0", "row1")]
         put(2, air_slots, h2[2], factor2)
         w1_low = [quantise_w1(w1_raw[0, 0], "w1_00", "grouped0")]

from contextlib import ExitStack

import concourse.mybir as mybir
from concourse.masks import make_identity

K, K2, H, N, T, S, T2, R = 1024, 512, 1024, 512, 2048, 512, 2048, 1024
FLOPS = 2 * (K * H * S + K2 * H * S + H * N * R)

F32 = mybir.dt.float32
BF16 = mybir.dt.bfloat16
I32 = mybir.dt.int32
U32 = mybir.dt.uint32
U16 = mybir.dt.uint16
U8 = mybir.dt.uint8
FP8X4 = mybir.dt.float8_e4m3fn_x4
FP4X4 = mybir.dt.float4_e2m1fn_x4
ACT = mybir.ActivationFunctionType
MULT = mybir.AluOpType.mult

P = 128
PACK = 4
PASS = P * PACK
SLICES = H // P
CUTS = (0, 256, 512, 768, 1024)
CHUNKS = len(CUTS) - 1
BANK = 512
ALIGN = 64
STAGE_TAGS = ("page0", "page1", "page2", "page3", "page4", "page6", "row6", "row7")


def tile_list_sleep_night_page_kernel(
    tc, tab_words, tab_scales, offs, tab2_words, tab2_scales, offs2, offs3, offs4, offs5,
    w1, gain, w2_words, w2_scales, wg1, wg2, page0, bias, w3, out,
):
    nc = tc.nc
    with ExitStack() as ctx:
        lists = ctx.enter_context(tc.tile_pool(name="lists", bufs=1))
        sb = ctx.enter_context(tc.tile_pool(name="sb", bufs=1))
        ps = ctx.enter_context(tc.psum_pool(name="ps", bufs=1))

        def sbuf(shape, dtype, name, tag=None):
            return sb.tile(shape, dtype, name=name, tag=tag or name, align_bytes=ALIGN)

        def bank(k, name):
            return ps.tile([P, 512], F32, name=name, tag="bank%d" % k)

        def load_list(src, name):
            dst = lists.tile([P, src.shape[1]], U16, name=name, tag=name)
            nc.sync.dma_start(dst[:], src)
            return dst

        def zeroed_plane(width, name, engine):
            plane = sbuf([P, width], U8, name)
            engine.memset(plane[:].bitcast(I32), 0)
            return plane

        def load_plane(plane, scales, queue):
            rows = 4 * scales.shape[0]
            for q in range(4):
                queue.dma_start(
                    plane[32 * q : 32 * q + rows, :].bitcast(I32),
                    scales[:, 4 * q : 4 * q + 4, :].bitcast(I32),
                )

        def load_words(words, name):
            dst = sbuf([P, T], I32, name)
            nc.sync.dma_start(dst[:], words.rearrange("p t i -> p (t i)").bitcast(I32))
            return dst

        def load_page(s):
            b, t = divmod(s, PACK)
            dst = sbuf([P, T2], F32, "page%d" % s)
            nc.sync.dma_start(dst[:], page0[b * PASS + t : (b + 1) * PASS : PACK, :])
            return dst

        def load_weight(w, a, cols, name, tag):
            raw = sbuf([P, PACK, PASS], F32, name, tag)
            rows = w[a * PASS : (a + 1) * PASS, cols]
            nc.sync.dma_start(raw[:], rows.rearrange("(p j) c -> p j c", j=PACK))
            return raw

        def load_rows(src, name):
            dst = sbuf([P, S], F32, name)
            nc.sync.dma_start(dst[:], src)
            return dst

        def load_channels(vec, name):
            dst = sbuf([P, H // PASS, PACK], F32, name)
            nc.sync.dma_start(dst[:], vec.rearrange("(b p t) -> p b t", p=P, t=PACK))
            return dst

        def deal_factor(raw, name, tag):
            turned = bank(0, name + "_turned")
            for c in range(S // P):
                nc.tensor.transpose(turned[:, c * P : (c + 1) * P], raw[:, c * P : (c + 1) * P], ident[:])
            spread = sbuf([P, PACK, S // P, P], F32, name + "_spread", tag)
            return turned, spread

        def deal_slot(turned, spread, t, name, which):
            by_t = turned[:].rearrange("p (c m t) -> p t c m", c=S // P, t=PACK)
            nc.scalar.activation(
                spread[:, t].rearrange("p c (a m) -> p c a m", a=4),
                by_t[:, t].unsqueeze(2).broadcast_to([P, S // P, 4, 32]),
                ACT.Copy,
            )
            back = bank(which, name + "_back")
            for c in range(S // P):
                nc.tensor.transpose(back[:, c * P : (c + 1) * P], spread[:, t, c, :], ident[:])
            dealt = sbuf([P, S], F32, name)
            nc.scalar.copy(dealt[:], back[:])
            return dealt

        def gather_words(table, offsets, name, tag=None):
            dst = sbuf([P, S], U32, name, tag)
            nc.vector.tensor_copy(dst[:], table[:].bitcast(U32).indirect(offsets[:]))
            return dst

        def gather_plane(plane, offsets, name, tag=None):
            dst = sbuf([P, S], U8, name, tag)
            nc.vector.tensor_copy(dst[:], plane[:].indirect(offsets[:]))
            return dst

        def quantise(grouped, name, tag=None):
            width = grouped.shape[1] // PACK
            codes = sbuf([P, width], U32, name + "_codes", tag)
            plane = sbuf([P, width], U8, name + "_plane")
            nc.vector.quantize_mx(out=codes[:].bitcast(FP8X4), scales=plane[:], in_=grouped[:])
            return codes, plane

        def quantise_w1(raw, name, tag):
            grouped = sbuf([P, PACK * PASS], BF16, name + "_grouped", tag)
            nc.scalar.copy(
                grouped[:].rearrange("p (t m j) -> p m t j", t=PACK, j=PACK),
                raw[:].rearrange("p j (m t) -> p m t j", t=PACK),
            )
            return quantise(grouped, name)

        def quantise_w3(raw, name, tag):
            grouped = sbuf([P, PACK * N], BF16, name + "_grouped", tag)
            nc.scalar.copy(
                grouped[:].rearrange("p (c i j) -> p c j i", i=4, j=PACK),
                raw[:].rearrange("p j (c i) -> p c j i", i=4),
            )
            return quantise(grouped, name)

        def airflow_features(s):
            acc = bank(5 + s % 3, "acc2_%d" % s)
            nc.tensor.matmul_mx(
                out=acc[:],
                lhsT=w2_codes[:, 2 * s * P : 2 * (s + 1) * P].bitcast(FP4X4),
                lhsT_scale=w2_plane[s % PACK][:, s // PACK, :],
                rhs=v2_codes[:].bitcast(FP8X4),
                rhs_scale=v2_plane[:],
                start=True,
                stop=True,
            )
            h2 = sbuf([P, S], F32, "h2_%d" % s, "row%d" % s)
            nc.scalar.activation(h2[:], acc[:], ACT.Abs)
            return h2

        def eeg_bounded(s, w1_q):
            t = s % PACK
            acc = bank(5 + s % 3, "acc1_%d" % s)
            for a in range(K // PASS):
                codes, plane = w1_q[a]
                nc.tensor.matmul_mx(
                    out=acc[:],
                    lhsT=codes[:, t * P : (t + 1) * P].bitcast(FP8X4),
                    lhsT_scale=plane[:, t * P : (t + 1) * P],
                    rhs=v_codes[a][:].bitcast(FP8X4),
                    rhs_scale=v_plane[4 * a : P, :],
                    start=(a == 0),
                    stop=(a == K // PASS - 1),
                )
            bounded = sbuf([P, S], F32, "bounded%d" % s, "bounded%d" % (s % 2))
            nc.scalar.activation(bounded[:], acc[:], ACT.Tanh)
            return bounded

        def eeg_features(s, bounded, tag):
            b, t = divmod(s, PACK)
            h1 = sbuf([P, S], F32, "h1_%d" % s, tag)
            nc.scalar.activation(h1[:], bounded[:], ACT.Copy, scale=gains[:, b, t : t + 1])
            return h1

        def put(s, offsets, h, factor):
            nc.vector.tensor_tensor(pages[s][:].indirect(offsets[:]), h[:], factor[s % PACK][:], MULT)

        def fetch(s, tag):
            picked = sbuf([P, R], F32, "picked%d" % s, tag)
            nc.vector.tensor_copy(picked[:], pages[s][:].indirect(read_list[:]))
            return picked

        def add_bias(s, picked, grouped):
            b, t = divmod(s, PACK)
            nc.scalar.activation(
                grouped.rearrange("p (n t) -> p n t", t=PACK)[:, :, t],
                picked,
                ACT.Identity,
                bias=biases[:, b, t : t + 1],
            )

        def score(c, a, codes, plane):
            w_codes, w_plane = w3_q[a]
            width = CUTS[c + 1] - CUTS[c]
            per_bank = BANK // width
            for n in range(N // P):
                k, i = divmod(n, per_bank)
                if a == 0 and i == 0:
                    accs[c].append(bank(CUTS[c] // P + k, "score%d_%d" % (c, k)))
                nc.tensor.matmul_mx(
                    out=accs[c][k][:, i * width : (i + 1) * width],
                    lhsT=w_codes[:, n * P : (n + 1) * P].bitcast(FP8X4),
                    lhsT_scale=w_plane[:, n * P : (n + 1) * P],
                    rhs=codes.bitcast(FP8X4),
                    rhs_scale=plane,
                    start=(a == 0 and i == 0),
                    stop=(a == 1 and i == per_bank - 1),
                )

        v2_window = zeroed_plane(T, "v2_window", nc.gpsimd)
        w2_raw_plane = zeroed_plane(H, "w2_raw_plane", nc.vector)

        ident = sbuf([P, P], F32, "ident")
        make_identity(nc, ident[:])
        v_window = zeroed_plane(T, "v_window", nc.gpsimd)

        pages = [None] * SLICES
        low, high = slice(0, PASS), slice(PASS, H)
        w2_raw = sbuf([P, 2 * H], U8, "w2_raw")
        nc.sync.dma_start(w2_raw[:].bitcast(I32), w2_words[0].bitcast(I32))
        wg2_raw = load_rows(wg2, "wg2_raw")
        load_plane(v2_window, tab2_scales, nc.sync)
        air_list = load_list(offs2, "air_list")
        v2_table = load_words(tab2_words[0], "v2_table")
        load_plane(w2_raw_plane, w2_scales, nc.sync)
        eeg_list = load_list(offs, "eeg_list")
        pages[0] = load_page(0)
        air_slots = load_list(offs4, "air_slots")
        pages[1] = load_page(1)
        load_plane(v_window, tab_scales, nc.gpsimd)
        v_table = [load_words(tab_words[0], "v_table0")]
        pages[2] = load_page(2)
        w1_raw = {(0, 0): load_weight(w1, 0, low, "w1_raw00", "raw0")}
        pages[3] = load_page(3)
        w1_raw[1, 0] = load_weight(w1, 1, low, "w1_raw10", "raw1")
        wg1_raw = load_rows(wg1, "wg1_raw")
        gains = load_channels(gain, "gains")
        v_table.append(load_words(tab_words[1], "v_table1"))
        eeg_slots = load_list(offs3, "eeg_slots")
        pages[4] = load_page(4)
        read_list = load_list(offs5, "read_list")
        biases = load_channels(bias, "biases")
        pages[5] = load_page(5)

        turned, spread = deal_factor(wg2_raw, "wg2", "raw2")
        w2_codes = sbuf([P, 2 * H], U8, "w2_codes")
        nc.vector.tensor_copy(
            w2_codes[:].bitcast(U16).rearrange("p (b t m) -> p b t m", t=PACK, m=P),
            w2_raw[:].bitcast(U16).rearrange("p (b m t) -> p b t m", t=PACK, m=P),
        )
        v2_plane = gather_plane(v2_window, air_list, "v2_plane")
        v2_codes = gather_words(v2_table, air_list, "v2_codes")
        by_slot = w2_raw_plane[:].rearrange("p (b m t) -> p b t m", t=PACK, m=P)
        w2_plane = [sbuf([P, H // PASS, P], U8, "w2_plane%d" % t) for t in range(PACK)]
        for t in range(PACK):
            nc.vector.tensor_copy(w2_plane[t][:], by_slot[:, :, t, :])
        v_plane = gather_plane(v_window, eeg_list, "v_plane")
        factor2, h2 = [], []
        for s in range(SLICES):
            if s < PACK:
                factor2.append(deal_slot(turned, spread, s, "factor2_%d" % s, 4 + s))
            h2.append(airflow_features(s))

        w1_raw[0, 1] = load_weight(w1, 0, high, "w1_raw01", "raw2")
        w1_raw[1, 1] = load_weight(w1, 1, high, "w1_raw11", "raw3")

        put(0, air_slots, h2[0], factor2)
        put(1, air_slots, h2[1], factor2)
        v_codes = [gather_words(v_table[0], eeg_list, "v_codes0", "row1")]
        put(2, air_slots, h2[2], factor2)
        w1_low = [quantise_w1(w1_raw[0, 0], "w1_00", "grouped0")]
        put(3, air_slots, h2[3], factor2)
        w1_low.append(quantise_w1(w1_raw[1, 0], "w1_10", "grouped1"))
        turned, spread = deal_factor(wg1_raw, "wg1", "v2_table")
        factor1 = [deal_slot(turned, spread, t, "factor1_%d" % t, 1 + t) for t in range(PACK)]

        w3_raw = [load_weight(w3, 0, slice(0, N), "w3_raw0", "raw0")]
        pages[6] = load_page(6)
        w3_raw.append(load_weight(w3, 1, slice(0, N), "w3_raw1", "raw1"))
        pages[7] = load_page(7)

        v_codes.append(gather_words(v_table[1], eeg_list, "v_codes1", "row2"))
        h1 = [eeg_features(s, eeg_bounded(s, w1_low), ("spare0", "row3", "spare1")[s]) for s in range(3)]
        bounded = eeg_bounded(3, w1_low)
        put(4, air_slots, h2[4], factor2)
        put(5, air_slots, h2[5], factor2)
        for s in range(3):
            put(s, eeg_slots, h1[s], factor1)
        w1_high = [
            quantise_w1(w1_raw[a, 1], "w1_%d1" % a, "grouped%d" % a) for a in range(K // PASS)
        ]
        h1.append(eeg_features(3, bounded, "grouped0"))
        picked = {0: fetch(0, "raw3")}
        w3_q = [quantise_w3(w3_raw[a], "w3_%d" % a, "v_table%d" % a) for a in range(H // PASS)]
        h1.extend([eeg_features(s, eeg_bounded(s, w1_high), ("row4", "row5", "row1")[s - 4]) for s in range(4, 7)])
        bounded = eeg_bounded(7, w1_high)
        put(3, eeg_slots, h1[3], factor1)
        picked[1] = fetch(1, "page0")
        put(6, air_slots, h2[6], factor2)

        low_parts = [((0,), "raw1"), ((1,), "raw0"), ((2, 3), "raw2")]
        low_cuts = [(CUTS[part[0]], CUTS[part[-1] + 1]) for part, tag in low_parts]
        x_low = [
            sbuf([P, PACK * (hi - lo)], BF16, "x_low%d" % lo, tag)
            for (lo, hi), (part, tag) in zip(low_cuts, low_parts)
        ]
        x_high = [sbuf([P, PACK * (CUTS[c + 1] - CUTS[c])], BF16, "x_high%d" % c) for c in range(CHUNKS)]
        accs = [[] for c in range(CHUNKS)]

        def bias_low(s):
            for (lo, hi), grouped in zip(low_cuts, x_low):
                add_bias(s, picked[s][:, lo:hi], grouped[:])

        def score_low(u, tag):
            lo = low_cuts[u][0]
            codes, plane = quantise(x_low[u], "x_low%d" % lo, tag)
            for c in low_parts[u][0]:
                cols = slice(CUTS[c] - lo, CUTS[c + 1] - lo)
                score(c, 0, codes[:, cols], plane[:, cols])

        def bias_high(s):
            for c in range(CHUNKS):
                add_bias(s, picked[s][:, CUTS[c] : CUTS[c + 1]], x_high[c][:])

        bias_low(0)
        bias_low(1)
        put(4, eeg_slots, h1[4], factor1)
        picked[2] = fetch(2, "page1")
        bias_low(2)
        put(5, eeg_slots, h1[5], factor1)
        picked[3] = fetch(3, "page2")
        bias_low(3)
        put(6, eeg_slots, h1[6], factor1)
        picked[4] = fetch(4, "page3")
        bias_high(4)
        put(7, air_slots, h2[7], factor2)
        score_low(0, "raw3")
        score_low(1, "v2_table")
        picked[5] = fetch(5, "page2")
        h1.append(eeg_features(7, bounded, "page5"))
        bias_high(5)
        picked[6] = fetch(6, "page3")
        bias_high(6)
        put(7, eeg_slots, h1[7], factor1)
        score_low(2, "bounded1")

        last = SLICES - 1
        out_rows = out.rearrange("(n p) j -> p n j", p=P)

        def fetch_last(c, tag):
            got = sbuf([P, CUTS[c + 1] - CUTS[c]], F32, "picked_last_%d" % c, tag)
            part = read_list[:, CUTS[c] // 16 : CUTS[c + 1] // 16]
            nc.vector.tensor_copy(got[:], pages[last][:].indirect(part))
            add_bias(last, got[:], x_high[c][:])

        def score_high(c):
            codes, plane = quantise(x_high[c], "x_high%d" % c)
            score(c, 1, codes[:], plane[:])

        def store(c):
            per_bank = (N // P) // len(accs[c])
            for k, acc in enumerate(accs[c]):
                which = CUTS[c] // P + k
                staged = sbuf([P, BANK], F32, "staged%d" % which, STAGE_TAGS[which])
                if which % 2 == 1:
                    nc.scalar.copy(staged[:], acc[:])
                else:
                    nc.vector.tensor_copy(staged[:], acc[:])
                nc.sync.dma_start(
                    out_rows[:, k * per_bank : (k + 1) * per_bank, CUTS[c] : CUTS[c + 1]],
                    staged[:].rearrange("p (i j) -> p i j", i=per_bank),
                )

        for c in range(CHUNKS - 1):
            fetch_last(c, "picked_last%d" % c)
        score_high(0)
        fetch_last(CHUNKS - 1, "picked_last0")
        store(0)
        for c in range(1, CHUNKS):
            score_high(c)
            store(c)
